import numpy as np, ml_dtypes
CORES = [3,0,2,1,6,7,4,5]
N = 8
def setup_inputs(rng):
    return {"x": rng.standard_normal((N, 128, 8), dtype=np.float32).astype(ml_dtypes.bfloat16)}
def reference(x):
    g = np.concatenate(list(x), axis=1)
    return {"y": np.broadcast_to(g, (N,) + g.shape)}

from concourse.bass import DstId, RemoteDMATransfer

W = 8
RANKS = 8
ENGINES = 16

SCRATCH = {
    "land": ("sbuf", [128, W * RANKS], "bfloat16"),
}
SEMAPHORES = ["loaded", "read", "arrived", "stored"]


def rank_program(g, core, T, topo):
    rank = T.rank_of(core)
    if rank is None:
        return
    mine = T.land[:, W * rank:W * (rank + 1)]
    peers = [c for c in T.cores if c != core]

    g.dma_start(mine, T.x[:]).then_inc(T.sem.loaded, 16)
    g.wait_ge(T.sem.loaded, 16)

    ids = []
    for p in peers:
        a = topo.addr(p)
        ids.append(DstId(rid=a[0], pnc=a[1]))
    g.remote_dma_fused(
        [RemoteDMATransfer(
            dst_ids=ids,
            dma_engine_mask=topo.mask(core, peers[0]),
            remote_sem=T.sem.arrived,
            srcs=[mine],
            dsts=[mine for p in peers],
            alu_op=0,
        )],
        local_sem=T.sem.read,
    )

    g.wait_ge(T.sem.arrived, ENGINES * len(peers))
    g.dma_start(T.y[:], T.land[:]).then_inc(T.sem.stored, 16)
    g.wait_ge(T.sem.read, ENGINES)
    g.wait_ge(T.sem.stored, 16)
